import numpy as np
import ml_dtypes


def mxq(x, axis, fmt="e4m3"):
    dtype, down = {"e4m3": (ml_dtypes.float8_e4m3fn, 7), "e5m2": (ml_dtypes.float8_e5m2, 14)}[fmt]
    v = np.moveaxis(np.asarray(x, np.float32).astype(ml_dtypes.bfloat16).astype(np.float64), axis, -1)
    blocks = v.reshape(v.shape[:-1] + (-1, 32))
    amax = np.abs(blocks).max(-1, keepdims=True)
    byte = np.maximum(np.where(amax > 0, np.frexp(amax)[1] - 1 + 127, 0) - down, 1)
    scale = np.exp2(byte - 127.0)
    codes = (blocks / scale).astype(np.float32).astype(dtype).astype(np.float64)
    return np.moveaxis((codes * scale).reshape(v.shape), -1, axis)


WIDE = False


def mx_kscale(k):
    if not WIDE:
        return np.ones(k)
    levels = np.array([10, -10, 5, -5, 0])
    if k % 512:
        return np.exp2(np.random.permutation(np.resize(levels, k // 32))).repeat(32)
    a = np.empty((k // 512, 16))
    for p in range(k // 512):
        a[p, :8] = np.random.permutation(np.resize(levels, 8))
        for g in range(8):
            far = levels[np.abs(levels - a[p, g]) >= 10]
            a[p, g + 8] = far[np.random.randint(len(far))]
    return np.exp2(a.ravel()).repeat(32)


def f64(x):
    return np.asarray(x).astype(np.float64)


def striped(idx):
    return np.tile(idx.reshape(-1, 16).T, (8, 1)).astype(np.uint16)


def unstriped(offs):
    return offs[:16].T.reshape(-1).astype(np.int64)


E2M1 = np.array([0.0, 0.5, 1.0, 1.5, 2.0, 3.0, 4.0, 6.0, -0.0, -0.5, -1.0, -1.5, -2.0, -3.0, -4.0, -6.0])


def pack_weight(w, fmt):
    k, n = w.shape
    w = f64(np.asarray(w, np.float32).astype(ml_dtypes.bfloat16)).reshape(k // 32, 32, n)
    amax = np.abs(w).max(1)
    if fmt == "e4m3":
        byte = np.frexp(amax)[1] - 1 + 127 - 7
    else:
        mant, ex = np.frexp(amax / 6.0)
        byte = np.where(mant > 0.5, ex, ex - 1) + 127
    byte = np.clip(np.where(amax > 0, byte, 1), 1, 254)
    scaled = (w * np.exp2(127.0 - byte)[:, None, :]).reshape(k, n).astype(np.float32)
    by_word = np.ascontiguousarray(scaled.reshape(k // 512, 128, 4, n).transpose(0, 1, 3, 2))
    if fmt == "e4m3":
        words = by_word.astype(ml_dtypes.float8_e4m3fn).view(np.uint8)
    else:
        c = by_word.astype(ml_dtypes.float4_e2m1fn).view(np.uint8) & 0xF
        words = (c[..., 0::2] | (c[..., 1::2] << 4)).reshape(k // 512, 128, 2 * n)
    return np.ascontiguousarray(words), np.ascontiguousarray(byte.astype(np.uint8).reshape(k // 512, 16, n))


def unpack_weight(words, scales, fmt):
    g, _, n = scales.shape
    words = np.ascontiguousarray(words).reshape(g, 128, n, -1)
    if fmt == "e4m3":
        vals = words.view(ml_dtypes.float8_e4m3fn).astype(np.float64)
    else:
        nib = np.empty((g, 128, n, 4), np.uint8)
        nib[..., 0::2] = words & 0xF
        nib[..., 1::2] = words >> 4
        vals = E2M1[nib]
    vals = vals * np.repeat(np.exp2(scales.astype(np.float64) - 127.0), 8, axis=1)[..., None]
    return vals.transpose(0, 1, 3, 2).reshape(g * 512, n)


def gelu(v):
    return 0.5 * v * (1.0 + np.tanh(np.sqrt(2.0 / np.pi) * (v + 0.044715 * v**3)))


K, KA, H, T, S, T3, S2, P = 1024, 512, 1024, 4096, 1024, 2048, 512, 512

def setup_inputs():
    n = np.random.standard_normal
    s = mx_kscale(K)[:, None]
    u = mx_kscale(H)[:, None]
    tab_words, tab_scales = pack_weight(n((K, T)) * s, "e4m3")
    tab2_words, tab2_scales = pack_weight(n((H, T3)) / np.sqrt(H) / u, "e4m3")
    w4_words, w4_scales = pack_weight(1.4 * n((KA, H)) / np.sqrt(K) / s[:KA], "e2m1")
    w1 = (1.4 * n((K - KA, H)) / np.sqrt(K) / s[KA:]).astype(np.float32)
    gain = (np.exp(0.4 * n(H)) * u[:, 0]).astype(np.float32)
    d = np.exp(0.4 * n(H)).astype(np.float32)
    ref = n((S2, P)).astype(np.float32)
    perm = np.random.permutation(S)
    return {"tab_words": tab_words, "tab_scales": tab_scales,
            "tab2_words": tab2_words, "tab2_scales": tab2_scales,
            "w4_words": w4_words, "w4_scales": w4_scales, "w1": w1,
            "gain": gain, "d": d, "ref": ref,
            "offs": striped(np.random.permutation(T)[:S]),
            "offs2": striped(np.random.permutation(T3)[:S2]),
            "pos1": striped(perm[:P]), "pos2": striped(perm[P:2 * P])}

def reference(tab_words, tab_scales, tab2_words, tab2_scales, w4_words, w4_scales, w1,
              gain, d, ref, offs, offs2, pos1, pos2):
    v = unpack_weight(tab_words, tab_scales, "e4m3")[:, unstriped(offs)]
    v2 = unpack_weight(tab2_words, tab2_scales, "e4m3")[:, unstriped(offs2)]
    w4 = unpack_weight(w4_words, w4_scales, "e2m1")
    w1q = mxq(f64(w1), 0, "e4m3")
    z = w4.T @ v[:KA] + w1q.T @ v[KA:]
    h = f64(gain)[:, None] * np.tanh(z)
    handle = h[:, unstriped(pos1)]
    x1 = f64(d)[:, None] * handle
    x2 = h[:, unstriped(pos2)] - handle
    x1q = mxq(x1, 0, "e4m3")
    x2q = mxq(x2, 0, "e4m3")
    e1 = v2.T @ x1q
    e2 = v2.T @ x2q
    return e1 * f64(ref) + e2

@@ -1,0 +1,278 @@
+from contextlib import ExitStack
+
+import concourse.mybir as mybir
+
+F32 = mybir.dt.float32
+BF16 = mybir.dt.bfloat16
+I32 = mybir.dt.int32
+U32 = mybir.dt.uint32
+U16 = mybir.dt.uint16
+U8 = mybir.dt.uint8
+FP8X4 = mybir.dt.float8_e4m3fn_x4
+FP4X4 = mybir.dt.float4_e2m1fn_x4
+ACT = mybir.ActivationFunctionType
+ALU = mybir.AluOpType
+
+P = 128
+PACK = 4
+H, T, S, T3, S2, N = 1024, 4096, 1024, 2048, 512, 512
+HALF = 512
+BANK = 512
+CHUNKS = ((0, 256), (256, 128), (384, 128))
+GAIN_ON_VECTOR = ((0, 0), (1, 0), (1, 1))
+
+FLOPS = 2 * 1024 * H * S + 2 * 2 * H * S2 * N
+
+
+def tile_list_handbag_authenticity_evidence_kernel(
+    tc, tab_words, tab_scales, tab2_words, tab2_scales, w4_words, w4_scales, w1, gain, d, ref,
+    offs, offs2, pos1, pos2, out,
+):
+    nc = tc.nc
+    with ExitStack() as ctx:
+        lists = ctx.enter_context(tc.tile_pool(name="lists", bufs=1))
+        keep = ctx.enter_context(tc.tile_pool(name="keep", bufs=1))
+        psum = ctx.enter_context(tc.psum_pool(name="psum", bufs=1))
+
+        def sb(name, shape, dtype, tag=None):
+            return keep.tile(shape, dtype, name=name, tag=tag or name, align_bytes=64)
+
+        def bank(i, name):
+            return psum.tile([P, BANK], F32, name=name, tag="bank%d" % i)
+
+        offs_t = lists.tile([P, S // 16], U16, name="offs_t")
+        offs2_t = lists.tile([P, S2 // 16], U16, name="offs2_t")
+        pos1_t = lists.tile([P, N // 16], U16, name="pos1_t")
+        pos2_t = lists.tile([P, N // 16], U16, name="pos2_t")
+
+        tab_plane = sb("tab_plane", [P, T], U8)
+        w4_plane_raw = sb("w4_plane_raw", [P, H], U8)
+        tab2_plane = sb("tab2_plane", [P, T3], U8)
+        for plane in (w4_plane_raw, tab_plane, tab2_plane):
+            nc.vector.memset(plane[:].bitcast(I32), 0)
+
+        tab_t = [sb("tab%d" % a, [P, T], I32) for a in range(2)]
+        tab2_t = [sb("tab2_%d" % a, [P, T3], I32) for a in range(2)]
+        w4_raw = sb("w4_raw", [P, H // 2], I32)
+        w1_raw = [sb("w1_raw%d" % b, [P, PACK, HALF], F32) for b in range(2)]
+        ref_t = sb("ref_t", [P, 4, N], F32)
+        gain_t = sb("gain_t", [P, 2, PACK], F32)
+        d_t = sb("d_t", [P, 2, PACK], F32)
+
+        def words(table, a):
+            return table[a].rearrange("p n t -> p (n t)").bitcast(I32)
+
+        w1_rows = w1.rearrange("(p j) c -> p j c", j=PACK)
+        def load_plane(queue, plane, scales):
+            passes = scales.shape[0]
+            for q in range(4):
+                queue.dma_start(
+                    out=plane[32 * q : 32 * q + 4 * passes, :].bitcast(I32),
+                    in_=scales[:, 4 * q : 4 * q + 4, :].bitcast(I32),
+                )
+
+        nc.scalar.dma_start(out=gain_t[:], in_=gain.rearrange("(b p t) -> p b t", b=2, t=PACK))
+        nc.scalar.dma_start(out=d_t[:], in_=d.rearrange("(b p t) -> p b t", b=2, t=PACK))
+        load_plane(nc.scalar, w4_plane_raw, w4_scales)
+        load_plane(nc.gpsimd, tab_plane, tab_scales)
+        nc.sync.dma_start(out=offs_t[:], in_=offs)
+        nc.sync.dma_start(out=w4_raw[:], in_=w4_words[0].bitcast(I32))
+        nc.sync.dma_start(out=tab_t[0][:], in_=words(tab_words, 0))
+        nc.sync.dma_start(out=tab_t[1][:], in_=words(tab_words, 1))
+        nc.sync.dma_start(out=w1_raw[0][:], in_=w1_rows[:, :, 0:HALF])
+        nc.sync.dma_start(out=pos1_t[:], in_=pos1)
+        nc.sync.dma_start(out=pos2_t[:], in_=pos2)
+        nc.sync.dma_start(out=w1_raw[1][:], in_=w1_rows[:, :, HALF:H])
+        nc.sync.dma_start(out=offs2_t[:], in_=offs2)
+        load_plane(nc.sync, tab2_plane, tab2_scales)
+        nc.sync.dma_start(out=tab2_t[0][:], in_=words(tab2_words, 0))
+        nc.sync.dma_start(out=tab2_t[1][:], in_=words(tab2_words, 1))
+        nc.sync.dma_start(out=ref_t[:], in_=ref.rearrange("(m p) n -> p m n", p=P))
+
+        w4_codes = sb("w4_codes", [P, H], U16)
+        nc.vector.tensor_copy(
+            out=w4_codes[:].rearrange("p (b t m) -> p b m t", b=2, t=PACK),
+            in_=w4_raw[:].bitcast(U16).rearrange("p (b m t) -> p b m t", b=2, t=PACK),
+        )
+        w4_plane = sb("w4_plane", [P, H], U8)
+        nc.vector.tensor_copy(
+            out=w4_plane[:].rearrange("p (b t m) -> p b m t", b=2, t=PACK),
+            in_=w4_plane_raw[:].rearrange("p (b m t) -> p b m t", b=2, t=PACK),
+        )
+        v_plane = sb("v_plane", [P, S], U8, tag="w4_plane_raw")
+        nc.vector.tensor_copy(out=v_plane[:], in_=tab_plane[:].indirect(offs_t[:]))
+        v_codes = []
+        for a, tag in enumerate(("tab_plane", "tab0")):
+            v_codes.append(sb("v_codes%d" % a, [P, S], U32, tag=tag))
+            nc.vector.tensor_copy(out=v_codes[a][:], in_=tab_t[a][:].bitcast(U32).indirect(offs_t[:]))
+
+        w1_codes, w1_plane = {}, {}
+
+        def quantise_w1(b):
+            grouped = sb("w1_grouped%d" % b, [P, 2, 2 * P * PACK], BF16, tag="tab1")
+            for u in range(2):
+                nc.vector.tensor_copy(
+                    out=grouped[:, u, :].rearrange("p (t m j) -> p m t j", t=2, j=PACK),
+                    in_=w1_raw[b][:].rearrange("p j (m t) -> p m t j", t=PACK)[:, :, 2 * u : 2 * u + 2, :],
+                )
+                w1_codes[b, u] = sb("w1_codes%d%d" % (b, u), [P, 2 * P], U32)
+                w1_plane[b, u] = sb("w1_plane%d%d" % (b, u), [P, 2 * P], U8)
+                nc.vector.quantize_mx(
+                    out=w1_codes[b, u][:].bitcast(FP8X4), scales=w1_plane[b, u][:], in_=grouped[:, u, :]
+                )
+
+        z, h = {}, {}
+
+        def w4_pass(b, t):
+            cols = slice(HALF * b + P * t, HALF * b + P * (t + 1))
+            for s in range(2):
+                z[b, t, s] = bank(2 * t + s, "z%d%d%d" % (b, t, s))
+                views = slice(BANK * s, BANK * (s + 1))
+                nc.tensor.matmul_mx(
+                    out=z[b, t, s][:], lhsT=w4_codes[:, cols].bitcast(FP4X4), lhsT_scale=w4_plane[:, cols],
+                    rhs=v_codes[0][:, views].bitcast(FP8X4), rhs_scale=v_plane[:, views], start=True, stop=False,
+                )
+
+        def w1_pass(b, t):
+            cols = slice(P * (t % 2), P * (t % 2 + 1))
+            for s in range(2):
+                views = slice(BANK * s, BANK * (s + 1))
+                nc.tensor.matmul_mx(
+                    out=z[b, t, s][:], lhsT=w1_codes[b, t // 2][:, cols].bitcast(FP8X4),
+                    lhsT_scale=w1_plane[b, t // 2][:, cols],
+                    rhs=v_codes[1][:, views].bitcast(FP8X4), rhs_scale=v_plane[4:P, views], start=False, stop=True,
+                )
+
+        def evidence(b, t):
+            h[b, t] = sb("h%d%d" % (b, t), [P, S], F32)
+            g = gain_t[:, b, t : t + 1]
+            for s in range(2):
+                views = slice(BANK * s, BANK * (s + 1))
+                nc.scalar.activation(out=h[b, t][:, views], in_=z[b, t, s][:], func=ACT.Tanh)
+                if (b, t) == (0, 0):
+                    nc.vector.tensor_scalar(out=h[b, t][:, views], in0=h[b, t][:, views], scalar1=g, scalar2=None, op0=ALU.mult)
+            if (b, t) == (0, 0):
+                return
+            if (b, t) in GAIN_ON_VECTOR:
+                nc.vector.tensor_scalar(out=h[b, t][:], in0=h[b, t][:], scalar1=g, scalar2=None, op0=ALU.mult)
+            else:
+                nc.scalar.activation(out=h[b, t][:], in_=h[b, t][:], func=ACT.Copy, scale=g)
+
+        def pick(b, t, handle, lining, n0, width):
+            cols = slice(n0 // 16, (n0 + width) // 16)
+            nc.vector.tensor_copy(out=handle[:, t, :], in_=h[b, t][:].indirect(pos1_t[:, cols]))
+            nc.vector.tensor_tensor(
+                out=lining[:, t, :], in0=h[b, t][:].indirect(pos2_t[:, cols]), in1=handle[:, t, :], op=ALU.subtract
+            )
+
+        def weave(dst, src):
+            nc.scalar.copy(
+                out=dst[:].rearrange("p (c i t) -> p c t i", i=PACK, t=PACK),
+                in_=src[:].rearrange("p t (c i) -> p c t i", i=PACK),
+            )
+
+        def quantise(name, woven, width):
+            codes = sb(name + "_codes", [P, width], U32)
+            plane = sb(name + "_plane", [P, width], U8)
+            nc.vector.quantize_mx(out=codes[:].bitcast(FP8X4), scales=plane[:], in_=woven[:])
+            return codes, plane
+
+        def handle_operand(name, b, handle, width):
+            scaled = sb(name + "_scaled", [P, PACK, width], BF16)
+            for t in range(PACK):
+                nc.scalar.activation(out=scaled[:, t, :], in_=handle[:, t, :], func=ACT.Copy, scale=d_t[:, b, t : t + 1])
+            woven = sb(name + "_woven", [P, PACK * width], BF16)
+            weave(woven, scaled)
+            return quantise(name, woven, width)
+
+        def lining_operand(name, lining, width):
+            woven = sb(name + "_woven", [P, PACK * width], BF16)
+            weave(woven, lining)
+            return quantise(name, woven, width)
+
+        for t in range(PACK):
+            w4_pass(0, t)
+        for b in range(2):
+            quantise_w1(b)
+
+        handle0 = sb("handle0", [P, PACK, N], F32)
+        lining0 = sb("lining0", [P, PACK, N], F32)
+        for t in range(PACK):
+            w1_pass(0, t)
+            evidence(0, t)
+            pick(0, t, handle0, lining0, 0, N)
+        v2_plane = sb("v2_plane", [P, S2], U8, tag="h00")
+        nc.vector.tensor_copy(out=v2_plane[:], in_=tab2_plane[:].indirect(offs2_t[:]))
+        v2_codes = []
+        for a in range(2):
+            v2_codes.append(sb("v2_codes%d" % a, [P, S2], U32, tag="h0%d" % (a + 1)))
+            nc.vector.tensor_copy(out=v2_codes[a][:], in_=tab2_t[a][:].bitcast(U32).indirect(offs2_t[:]))
+
+        n0, width = CHUNKS[0]
+        handle1 = sb("handle1_0", [P, PACK, width], F32)
+        lining1 = sb("lining1_0", [P, PACK, width], F32)
+        for t in range(PACK):
+            w4_pass(1, t)
+            w1_pass(1, t)
+            evidence(1, t)
+            pick(1, t, handle1, lining1, n0, width)
+        picked = [(handle1, lining1)]
+
+        x1_0 = handle_operand("x1_0", 0, handle0, N)
+        reuse = ("handle0", "x2_0_woven")
+        x2_0 = None
+        for c in (1, 2):
+            if c == 2:
+                x2_0 = lining_operand("x2_0", lining0, N)
+            n0, width = CHUNKS[c]
+            handle1 = sb("handle1_%d" % c, [P, PACK, width], F32, tag=reuse[c - 1])
+            lining1 = sb("lining1_%d" % c, [P, PACK, width], F32)
+            for t in range(PACK):
+                pick(1, t, handle1, lining1, n0, width)
+            picked.append((handle1, lining1))
+
+        def score_pass(banks, a, x, cols, width, first):
+            codes, plane = x
+            per_bank = BANK // width
+            for m in range(4):
+                rows = slice(P * m, P * (m + 1))
+                k = m % per_bank
+                nc.tensor.matmul_mx(
+                    out=banks[m // per_bank][:, k * width : (k + 1) * width],
+                    lhsT=v2_codes[a][:, rows].bitcast(FP8X4), lhsT_scale=v2_plane[4 * a : P, rows],
+                    rhs=codes[:, cols].bitcast(FP8X4), rhs_scale=plane[:, cols],
+                    start=(first and k == 0), stop=(not first and k == per_bank - 1),
+                )
+
+        e1, e2 = [], []
+        first_bank = 0
+        for c, (n0, width) in enumerate(CHUNKS):
+            count = 4 * width // BANK
+            e1.append([bank(first_bank + i, "e1_%d%d" % (c, i)) for i in range(count)])
+            e2.append([bank(first_bank + count + i, "e2_%d%d" % (c, i)) for i in range(count)])
+            first_bank = first_bank + 2 * count
+        for c, (n0, width) in enumerate(CHUNKS):
+            score_pass(e1[c], 0, x1_0, slice(n0, n0 + width), width, True)
+        for c, (n0, width) in enumerate(CHUNKS):
+            score_pass(e2[c], 0, x2_0, slice(n0, n0 + width), width, True)
+
+        out_rows = out.rearrange("(m p) n -> p m n", p=P)
+        for c, (n0, width) in enumerate(CHUNKS):
+            handle1, lining1 = picked[c]
+            x1_1 = handle_operand("x1_1%d" % c, 1, handle1, width)
+            score_pass(e1[c], 1, x1_1, slice(0, width), width, False)
+            x2_1 = lining_operand("x2_1%d" % c, lining1, width)
+            score_pass(e2[c], 1, x2_1, slice(0, width), width, False)
+            per_bank = BANK // width
+            for i in range(len(e1[c])):
+                rows = slice(per_bank * i, per_bank * (i + 1))
+                weighted = sb("weighted%d%d" % (c, i), [P, per_bank, width], F32)
+                result = sb("result%d%d" % (c, i), [P, per_bank, width], F32)
+                nc.vector.tensor_tensor(
+                    out=weighted[:], in0=e1[c][i][:].rearrange("p (m n) -> p m n", n=width),
+                    in1=ref_t[:, rows, n0 : n0 + width], op=ALU.mult,
+                )
+                nc.vector.tensor_tensor(
+                    out=result[:], in0=e2[c][i][:].rearrange("p (m n) -> p m n", n=width), in1=weighted[:], op=ALU.add
+                )
+                nc.sync.dma_start(out=out_rows[:, rows, n0 : n0 + width], in_=result[:])

@@ -19,7 +19,7 @@ H, T, S, T3, S2, N = 1024, 4096, 1024, 2048, 512, 512
 HALF = 512
 BANK = 512
 CHUNKS = ((0, 256), (256, 128), (384, 128))
-GAIN_ON_VECTOR = ((0, 0), (1, 0), (1, 1))
+GAIN_ON_VECTOR = ((0, 0),)
 
 FLOPS = 2 * 1024 * H * S + 2 * 2 * H * S2 * N
 
@@ -48,7 +48,7 @@ def tile_list_handbag_authenticity_evidence_kernel(
         tab_plane = sb("tab_plane", [P, T], U8)
         w4_plane_raw = sb("w4_plane_raw", [P, H], U8)
         tab2_plane = sb("tab2_plane", [P, T3], U8)
-        for plane in (w4_plane_raw, tab_plane, tab2_plane):
+        for plane in (tab_plane, w4_plane_raw, tab2_plane):
             nc.vector.memset(plane[:].bitcast(I32), 0)
 
         tab_t = [sb("tab%d" % a, [P, T], I32) for a in range(2)]
@@ -71,20 +71,20 @@ def tile_list_handbag_authenticity_evidence_kernel(
                     in_=scales[:, 4 * q : 4 * q + 4, :].bitcast(I32),
                 )
 
-        nc.scalar.dma_start(out=gain_t[:], in_=gain.rearrange("(b p t) -> p b t", b=2, t=PACK))
-        nc.scalar.dma_start(out=d_t[:], in_=d.rearrange("(b p t) -> p b t", b=2, t=PACK))
-        load_plane(nc.scalar, w4_plane_raw, w4_scales)
         load_plane(nc.gpsimd, tab_plane, tab_scales)
+        load_plane(nc.gpsimd, w4_plane_raw, w4_scales)
+        load_plane(nc.gpsimd, tab2_plane, tab2_scales)
         nc.sync.dma_start(out=offs_t[:], in_=offs)
         nc.sync.dma_start(out=w4_raw[:], in_=w4_words[0].bitcast(I32))
         nc.sync.dma_start(out=tab_t[0][:], in_=words(tab_words, 0))
         nc.sync.dma_start(out=tab_t[1][:], in_=words(tab_words, 1))
         nc.sync.dma_start(out=w1_raw[0][:], in_=w1_rows[:, :, 0:HALF])
+        nc.sync.dma_start(out=gain_t[:], in_=gain.rearrange("(b p t) -> p b t", b=2, t=PACK))
         nc.sync.dma_start(out=pos1_t[:], in_=pos1)
         nc.sync.dma_start(out=pos2_t[:], in_=pos2)
-        nc.sync.dma_start(out=w1_raw[1][:], in_=w1_rows[:, :, HALF:H])
         nc.sync.dma_start(out=offs2_t[:], in_=offs2)
-        load_plane(nc.sync, tab2_plane, tab2_scales)
+        nc.sync.dma_start(out=w1_raw[1][:], in_=w1_rows[:, :, HALF:H])
+        nc.sync.dma_start(out=d_t[:], in_=d.rearrange("(b p t) -> p b t", b=2, t=PACK))
         nc.sync.dma_start(out=tab2_t[0][:], in_=words(tab2_words, 0))
         nc.sync.dma_start(out=tab2_t[1][:], in_=words(tab2_words, 1))
         nc.sync.dma_start(out=ref_t[:], in_=ref.rearrange("(m p) n -> p m n", p=P))
@@ -94,17 +94,17 @@ def tile_list_handbag_authenticity_evidence_kernel(
             out=w4_codes[:].rearrange("p (b t m) -> p b m t", b=2, t=PACK),
             in_=w4_raw[:].bitcast(U16).rearrange("p (b m t) -> p b m t", b=2, t=PACK),
         )
-        w4_plane = sb("w4_plane", [P, H], U8)
+        v_plane = sb("v_plane", [P, S], U8)
+        nc.vector.tensor_copy(out=v_plane[:], in_=tab_plane[:].indirect(offs_t[:]))
+        v_codes = [sb("v_codes0", [P, S], U32, tag="tab_plane")]
+        nc.vector.tensor_copy(out=v_codes[0][:], in_=tab_t[0][:].bitcast(U32).indirect(offs_t[:]))
+        w4_plane = sb("w4_plane", [P, H], U8, tag="tab0")
         nc.vector.tensor_copy(
             out=w4_plane[:].rearrange("p (b t m) -> p b m t", b=2, t=PACK),
             in_=w4_plane_raw[:].rearrange("p (b m t) -> p b m t", b=2, t=PACK),
         )
-        v_plane = sb("v_plane", [P, S], U8, tag="w4_plane_raw")
-        nc.vector.tensor_copy(out=v_plane[:], in_=tab_plane[:].indirect(offs_t[:]))
-        v_codes = []
-        for a, tag in enumerate(("tab_plane", "tab0")):
-            v_codes.append(sb("v_codes%d" % a, [P, S], U32, tag=tag))
-            nc.vector.tensor_copy(out=v_codes[a][:], in_=tab_t[a][:].bitcast(U32).indirect(offs_t[:]))
+        v_codes.append(sb("v_codes1", [P, S], U32, tag="w4_plane_raw"))
+        nc.vector.tensor_copy(out=v_codes[1][:], in_=tab_t[1][:].bitcast(U32).indirect(offs_t[:]))
 
         w1_codes, w1_plane = {}, {}
 
@@ -158,81 +158,57 @@ def tile_list_handbag_authenticity_evidence_kernel(
             else:
                 nc.scalar.activation(out=h[b, t][:], in_=h[b, t][:], func=ACT.Copy, scale=g)
 
-        def pick(b, t, handle, lining, n0, width):
-            cols = slice(n0 // 16, (n0 + width) // 16)
-            nc.vector.tensor_copy(out=handle[:, t, :], in_=h[b, t][:].indirect(pos1_t[:, cols]))
+        def pick(b, t):
+            nc.vector.tensor_copy(out=handle[b][:, t, :], in_=h[b, t][:].indirect(pos1_t[:]))
             nc.vector.tensor_tensor(
-                out=lining[:, t, :], in0=h[b, t][:].indirect(pos2_t[:, cols]), in1=handle[:, t, :], op=ALU.subtract
+                out=lining[b][:, t, :], in0=h[b, t][:].indirect(pos2_t[:]), in1=handle[b][:, t, :], op=ALU.subtract
             )
 
-        def weave(dst, src):
-            nc.scalar.copy(
-                out=dst[:].rearrange("p (c i t) -> p c t i", i=PACK, t=PACK),
-                in_=src[:].rearrange("p t (c i) -> p c t i", i=PACK),
+        def weave(copy, name, rows, width):
+            woven = sb(name + "_woven", [P, PACK * width], BF16)
+            copy(
+                out=woven[:].rearrange("p (c i t) -> p c t i", i=PACK, t=PACK),
+                in_=rows.rearrange("p t (c i) -> p c t i", i=PACK),
             )
-
-        def quantise(name, woven, width):
             codes = sb(name + "_codes", [P, width], U32)
             plane = sb(name + "_plane", [P, width], U8)
             nc.vector.quantize_mx(out=codes[:].bitcast(FP8X4), scales=plane[:], in_=woven[:])
             return codes, plane
 
-        def handle_operand(name, b, handle, width):
-            scaled = sb(name + "_scaled", [P, PACK, width], BF16)
+        def scale_handle(b):
+            scaled = sb("scaled%d" % b, [P, PACK, N], BF16)
             for t in range(PACK):
-                nc.scalar.activation(out=scaled[:, t, :], in_=handle[:, t, :], func=ACT.Copy, scale=d_t[:, b, t : t + 1])
-            woven = sb(name + "_woven", [P, PACK * width], BF16)
-            weave(woven, scaled)
-            return quantise(name, woven, width)
-
-        def lining_operand(name, lining, width):
-            woven = sb(name + "_woven", [P, PACK * width], BF16)
-            weave(woven, lining)
-            return quantise(name, woven, width)
+                nc.scalar.activation(
+                    out=scaled[:, t, :], in_=handle[b][:, t, :], func=ACT.Copy, scale=d_t[:, b, t : t + 1]
+                )
+            return scaled
 
         for t in range(PACK):
             w4_pass(0, t)
-        for b in range(2):
-            quantise_w1(b)
+        quantise_w1(0)
+        v2_plane = sb("v2_plane", [P, S2], U8, tag="w1_raw0")
+        nc.vector.tensor_copy(out=v2_plane[:], in_=tab2_plane[:].indirect(offs2_t[:]))
+        quantise_w1(1)
 
-        handle0 = sb("handle0", [P, PACK, N], F32)
-        lining0 = sb("lining0", [P, PACK, N], F32)
+        handle = [sb("handle%d" % b, [P, PACK, N], F32) for b in range(2)]
+        lining = [sb("lining%d" % b, [P, PACK, N], F32) for b in range(2)]
         for t in range(PACK):
             w1_pass(0, t)
             evidence(0, t)
-            pick(0, t, handle0, lining0, 0, N)
-        v2_plane = sb("v2_plane", [P, S2], U8, tag="h00")
-        nc.vector.tensor_copy(out=v2_plane[:], in_=tab2_plane[:].indirect(offs2_t[:]))
+            pick(0, t)
         v2_codes = []
         for a in range(2):
             v2_codes.append(sb("v2_codes%d" % a, [P, S2], U32, tag="h0%d" % (a + 1)))
             nc.vector.tensor_copy(out=v2_codes[a][:], in_=tab2_t[a][:].bitcast(U32).indirect(offs2_t[:]))
-
-        n0, width = CHUNKS[0]
-        handle1 = sb("handle1_0", [P, PACK, width], F32)
-        lining1 = sb("lining1_0", [P, PACK, width], F32)
         for t in range(PACK):
             w4_pass(1, t)
             w1_pass(1, t)
             evidence(1, t)
-            pick(1, t, handle1, lining1, n0, width)
-        picked = [(handle1, lining1)]
+            pick(1, t)
 
-        x1_0 = handle_operand("x1_0", 0, handle0, N)
-        reuse = ("handle0", "x2_0_woven")
-        x2_0 = None
-        for c in (1, 2):
-            if c == 2:
-                x2_0 = lining_operand("x2_0", lining0, N)
-            n0, width = CHUNKS[c]
-            handle1 = sb("handle1_%d" % c, [P, PACK, width], F32, tag=reuse[c - 1])
-            lining1 = sb("lining1_%d" % c, [P, PACK, width], F32)
-            for t in range(PACK):
-                pick(1, t, handle1, lining1, n0, width)
-            picked.append((handle1, lining1))
-
-        def score_pass(banks, a, x, cols, width, first):
+        def score_pass(banks, a, x, cols):
             codes, plane = x
+            width = cols.stop - cols.start
             per_bank = BANK // width
             for m in range(4):
                 rows = slice(P * m, P * (m + 1))
@@ -241,38 +217,36 @@ def tile_list_handbag_authenticity_evidence_kernel(
                     out=banks[m // per_bank][:, k * width : (k + 1) * width],
                     lhsT=v2_codes[a][:, rows].bitcast(FP8X4), lhsT_scale=v2_plane[4 * a : P, rows],
                     rhs=codes[:, cols].bitcast(FP8X4), rhs_scale=plane[:, cols],
-                    start=(first and k == 0), stop=(not first and k == per_bank - 1),
+                    start=(a == 0 and k == 0), stop=(a == 1 and k == per_bank - 1),
                 )
 
-        e1, e2 = [], []
-        first_bank = 0
+        e1 = [bank(m, "e1_%d" % m) for m in range(4)]
+        for b, copy in enumerate((nc.scalar.copy, nc.vector.tensor_copy)):
+            x1 = weave(copy, "x1_%d" % b, scale_handle(b)[:], N)
+            score_pass(e1, b, x1, slice(0, N))
+        weighted = sb("weighted", [P, 4, N], F32)
+        for m in range(4):
+            nc.vector.tensor_tensor(out=weighted[:, m, :], in0=e1[m][:], in1=ref_t[:, m, :], op=ALU.mult)
+
+        e2 = []
         for c, (n0, width) in enumerate(CHUNKS):
-            count = 4 * width // BANK
-            e1.append([bank(first_bank + i, "e1_%d%d" % (c, i)) for i in range(count)])
-            e2.append([bank(first_bank + count + i, "e2_%d%d" % (c, i)) for i in range(count)])
-            first_bank = first_bank + 2 * count
+            first = 4 + 4 * n0 // BANK
+            e2.append([bank(first + i, "e2_%d%d" % (c, i)) for i in range(4 * width // BANK)])
+        x2 = weave(nc.scalar.copy, "x2_0", lining[0][:], N)
         for c, (n0, width) in enumerate(CHUNKS):
-            score_pass(e1[c], 0, x1_0, slice(n0, n0 + width), width, True)
-        for c, (n0, width) in enumerate(CHUNKS):
-            score_pass(e2[c], 0, x2_0, slice(n0, n0 + width), width, True)
+            score_pass(e2[c], 0, x2, slice(n0, n0 + width))
 
         out_rows = out.rearrange("(m p) n -> p m n", p=P)
         for c, (n0, width) in enumerate(CHUNKS):
-            handle1, lining1 = picked[c]
-            x1_1 = handle_operand("x1_1%d" % c, 1, handle1, width)
-            score_pass(e1[c], 1, x1_1, slice(0, width), width, False)
-            x2_1 = lining_operand("x2_1%d" % c, lining1, width)
-            score_pass(e2[c], 1, x2_1, slice(0, width), width, False)
+            cols = slice(n0, n0 + width)
+            x2 = weave(nc.scalar.copy, "x2_1%d" % c, lining[1][:, :, cols], width)
+            score_pass(e2[c], 1, x2, slice(0, width))
             per_bank = BANK // width
-            for i in range(len(e1[c])):
+            for i in range(len(e2[c])):
                 rows = slice(per_bank * i, per_bank * (i + 1))
-                weighted = sb("weighted%d%d" % (c, i), [P, per_bank, width], F32)
                 result = sb("result%d%d" % (c, i), [P, per_bank, width], F32)
                 nc.vector.tensor_tensor(
-                    out=weighted[:], in0=e1[c][i][:].rearrange("p (m n) -> p m n", n=width),
-                    in1=ref_t[:, rows, n0 : n0 + width], op=ALU.mult,
+                    out=result[:], in0=e2[c][i][:].rearrange("p (m n) -> p m n", n=width),
+                    in1=weighted[:, rows, cols], op=ALU.add,
                 )
-                nc.vector.tensor_tensor(
-                    out=result[:], in0=e2[c][i][:].rearrange("p (m n) -> p m n", n=width), in1=weighted[:], op=ALU.add
-                )
-                nc.sync.dma_start(out=out_rows[:, rows, n0 : n0 + width], in_=result[:])
+                nc.sync.dma_start(out=out_rows[:, rows, cols], in_=result[:])

@@ -48,7 +48,7 @@ def tile_list_handbag_authenticity_evidence_kernel(
         tab_plane = sb("tab_plane", [P, T], U8)
         w4_plane_raw = sb("w4_plane_raw", [P, H], U8)
         tab2_plane = sb("tab2_plane", [P, T3], U8)
-        for plane in (tab_plane, w4_plane_raw, tab2_plane):
+        for plane in (w4_plane_raw, tab_plane, tab2_plane):
             nc.vector.memset(plane[:].bitcast(I32), 0)
 
         tab_t = [sb("tab%d" % a, [P, T], I32) for a in range(2)]
@@ -71,12 +71,11 @@ def tile_list_handbag_authenticity_evidence_kernel(
                     in_=scales[:, 4 * q : 4 * q + 4, :].bitcast(I32),
                 )
 
-        load_plane(nc.gpsimd, tab_plane, tab_scales)
-        load_plane(nc.gpsimd, w4_plane_raw, w4_scales)
-        load_plane(nc.gpsimd, tab2_plane, tab2_scales)
         nc.sync.dma_start(out=offs_t[:], in_=offs)
-        nc.sync.dma_start(out=w4_raw[:], in_=w4_words[0].bitcast(I32))
         nc.sync.dma_start(out=tab_t[0][:], in_=words(tab_words, 0))
+        load_plane(nc.sync, w4_plane_raw, w4_scales)
+        nc.sync.dma_start(out=w4_raw[:], in_=w4_words[0].bitcast(I32))
+        load_plane(nc.sync, tab_plane, tab_scales)
         nc.sync.dma_start(out=tab_t[1][:], in_=words(tab_words, 1))
         nc.sync.dma_start(out=w1_raw[0][:], in_=w1_rows[:, :, 0:HALF])
         nc.sync.dma_start(out=gain_t[:], in_=gain.rearrange("(b p t) -> p b t", b=2, t=PACK))
@@ -85,33 +84,34 @@ def tile_list_handbag_authenticity_evidence_kernel(
         nc.sync.dma_start(out=offs2_t[:], in_=offs2)
         nc.sync.dma_start(out=w1_raw[1][:], in_=w1_rows[:, :, HALF:H])
         nc.sync.dma_start(out=d_t[:], in_=d.rearrange("(b p t) -> p b t", b=2, t=PACK))
+        load_plane(nc.sync, tab2_plane, tab2_scales)
         nc.sync.dma_start(out=tab2_t[0][:], in_=words(tab2_words, 0))
         nc.sync.dma_start(out=tab2_t[1][:], in_=words(tab2_words, 1))
         nc.sync.dma_start(out=ref_t[:], in_=ref.rearrange("(m p) n -> p m n", p=P))
 
+        v_codes = [sb("v_codes0", [P, S], U32)]
+        nc.vector.tensor_copy(out=v_codes[0][:], in_=tab_t[0][:].bitcast(U32).indirect(offs_t[:]))
         w4_codes = sb("w4_codes", [P, H], U16)
-        nc.vector.tensor_copy(
+        nc.scalar.copy(
             out=w4_codes[:].rearrange("p (b t m) -> p b m t", b=2, t=PACK),
             in_=w4_raw[:].bitcast(U16).rearrange("p (b m t) -> p b m t", b=2, t=PACK),
         )
-        v_plane = sb("v_plane", [P, S], U8)
-        nc.vector.tensor_copy(out=v_plane[:], in_=tab_plane[:].indirect(offs_t[:]))
-        v_codes = [sb("v_codes0", [P, S], U32, tag="tab_plane")]
-        nc.vector.tensor_copy(out=v_codes[0][:], in_=tab_t[0][:].bitcast(U32).indirect(offs_t[:]))
-        w4_plane = sb("w4_plane", [P, H], U8, tag="tab0")
+        w4_plane = sb("w4_plane", [P, H], U8)
         nc.vector.tensor_copy(
             out=w4_plane[:].rearrange("p (b t m) -> p b m t", b=2, t=PACK),
             in_=w4_plane_raw[:].rearrange("p (b m t) -> p b m t", b=2, t=PACK),
         )
-        v_codes.append(sb("v_codes1", [P, S], U32, tag="w4_plane_raw"))
+        v_plane = sb("v_plane", [P, S], U8)
+        nc.vector.tensor_copy(out=v_plane[:], in_=tab_plane[:].indirect(offs_t[:]))
+        v_codes.append(sb("v_codes1", [P, S], U32, tag="tab_plane"))
         nc.vector.tensor_copy(out=v_codes[1][:], in_=tab_t[1][:].bitcast(U32).indirect(offs_t[:]))
 
         w1_codes, w1_plane = {}, {}
 
-        def quantise_w1(b):
+        def quantise_w1(b, copy):
             grouped = sb("w1_grouped%d" % b, [P, 2, 2 * P * PACK], BF16, tag="tab1")
             for u in range(2):
-                nc.vector.tensor_copy(
+                copy(
                     out=grouped[:, u, :].rearrange("p (t m j) -> p m t j", t=2, j=PACK),
                     in_=w1_raw[b][:].rearrange("p j (m t) -> p m t j", t=PACK)[:, :, 2 * u : 2 * u + 2, :],
                 )
@@ -158,8 +158,10 @@ def tile_list_handbag_authenticity_evidence_kernel(
             else:
                 nc.scalar.activation(out=h[b, t][:], in_=h[b, t][:], func=ACT.Copy, scale=g)
 
-        def pick(b, t):
+        def pick_handle(b, t):
             nc.vector.tensor_copy(out=handle[b][:, t, :], in_=h[b, t][:].indirect(pos1_t[:]))
+
+        def pick_lining(b, t):
             nc.vector.tensor_tensor(
                 out=lining[b][:, t, :], in0=h[b, t][:].indirect(pos2_t[:]), in1=handle[b][:, t, :], op=ALU.subtract
             )
@@ -185,17 +187,19 @@ def tile_list_handbag_authenticity_evidence_kernel(
 
         for t in range(PACK):
             w4_pass(0, t)
-        quantise_w1(0)
-        v2_plane = sb("v2_plane", [P, S2], U8, tag="w1_raw0")
-        nc.vector.tensor_copy(out=v2_plane[:], in_=tab2_plane[:].indirect(offs2_t[:]))
-        quantise_w1(1)
+        quantise_w1(0, nc.vector.tensor_copy)
 
         handle = [sb("handle%d" % b, [P, PACK, N], F32) for b in range(2)]
-        lining = [sb("lining%d" % b, [P, PACK, N], F32) for b in range(2)]
+        lining = [sb("lining0", [P, PACK, N], F32)]
         for t in range(PACK):
             w1_pass(0, t)
             evidence(0, t)
-            pick(0, t)
+            pick_handle(0, t)
+            pick_lining(0, t)
+            if t == 1:
+                quantise_w1(1, nc.scalar.copy)
+        v2_plane = sb("v2_plane", [P, S2], U8, tag="h00")
+        nc.vector.tensor_copy(out=v2_plane[:], in_=tab2_plane[:].indirect(offs2_t[:]))
         v2_codes = []
         for a in range(2):
             v2_codes.append(sb("v2_codes%d" % a, [P, S2], U32, tag="h0%d" % (a + 1)))
@@ -204,7 +208,11 @@ def tile_list_handbag_authenticity_evidence_kernel(
             w4_pass(1, t)
             w1_pass(1, t)
             evidence(1, t)
-            pick(1, t)
+            pick_handle(1, t)
+        scaled0 = scale_handle(0)
+        lining.append(sb("lining1", [P, PACK, N], F32, tag="handle0"))
+        for t in range(PACK):
+            pick_lining(1, t)
 
         def score_pass(banks, a, x, cols):
             codes, plane = x
@@ -221,9 +229,8 @@ def tile_list_handbag_authenticity_evidence_kernel(
                 )
 
         e1 = [bank(m, "e1_%d" % m) for m in range(4)]
-        for b, copy in enumerate((nc.scalar.copy, nc.vector.tensor_copy)):
-            x1 = weave(copy, "x1_%d" % b, scale_handle(b)[:], N)
-            score_pass(e1, b, x1, slice(0, N))
+        score_pass(e1, 0, weave(nc.scalar.copy, "x1_0", scaled0[:], N), slice(0, N))
+        score_pass(e1, 1, weave(nc.scalar.copy, "x1_1", scale_handle(1)[:], N), slice(0, N))
         weighted = sb("weighted", [P, 4, N], F32)
         for m in range(4):
             nc.vector.tensor_tensor(out=weighted[:, m, :], in0=e1[m][:], in1=ref_t[:, m, :], op=ALU.mult)

@@ -19,7 +19,6 @@ H, T, S, T3, S2, N = 1024, 4096, 1024, 2048, 512, 512
 HALF = 512
 BANK = 512
 CHUNKS = ((0, 256), (256, 128), (384, 128))
-GAIN_ON_VECTOR = ((0, 0),)
 
 FLOPS = 2 * 1024 * H * S + 2 * 2 * H * S2 * N
 
@@ -45,10 +44,15 @@ def tile_list_handbag_authenticity_evidence_kernel(
         pos1_t = lists.tile([P, N // 16], U16, name="pos1_t")
         pos2_t = lists.tile([P, N // 16], U16, name="pos2_t")
 
-        tab_plane = sb("tab_plane", [P, T], U8)
+        tab_rows = sb("tab_rows", [P, T], U8)
+        tab2_rows = sb("tab2_rows", [P, T3], U8)
         w4_plane_raw = sb("w4_plane_raw", [P, H], U8)
-        tab2_plane = sb("tab2_plane", [P, T3], U8)
-        for plane in (w4_plane_raw, tab_plane, tab2_plane):
+        v_plane = [sb("v_plane%d" % a, [P, S], U8) for a in range(2)]
+        v2_plane = sb("v2_plane", [P, S2], U8)
+        nc.vector.memset(w4_plane_raw[:].bitcast(I32), 0)
+        for rows in (tab_rows, tab2_rows):
+            nc.vector.memset(rows[0:96, :].bitcast(I32), 0)
+        for plane in (v_plane[0], v_plane[1], v2_plane):
             nc.vector.memset(plane[:].bitcast(I32), 0)
 
         tab_t = [sb("tab%d" % a, [P, T], I32) for a in range(2)]
@@ -63,63 +67,76 @@ def tile_list_handbag_authenticity_evidence_kernel(
             return table[a].rearrange("p n t -> p (n t)").bitcast(I32)
 
         w1_rows = w1.rearrange("(p j) c -> p j c", j=PACK)
-        def load_plane(queue, plane, scales):
-            passes = scales.shape[0]
+        def load_rows(rows, scales):
+            nc.sync.dma_start(out=rows[96:P, :].bitcast(I32), in_=scales.rearrange("a q t -> (a q) t").bitcast(I32))
+
+        def place_rows(plane, picked, a):
             for q in range(4):
-                queue.dma_start(
-                    out=plane[32 * q : 32 * q + 4 * passes, :].bitcast(I32),
-                    in_=scales[:, 4 * q : 4 * q + 4, :].bitcast(I32),
+                nc.sync.dma_start(
+                    out=plane[32 * q + 4 * a : 32 * q + 4 * a + 4, :].bitcast(I32),
+                    in_=picked[96 + 16 * a + 4 * q : 96 + 16 * a + 4 * q + 4, :].bitcast(I32),
                 )
 
         nc.sync.dma_start(out=offs_t[:], in_=offs)
-        nc.sync.dma_start(out=tab_t[0][:], in_=words(tab_words, 0))
-        load_plane(nc.sync, w4_plane_raw, w4_scales)
+        load_rows(tab_rows, tab_scales)
         nc.sync.dma_start(out=w4_raw[:], in_=w4_words[0].bitcast(I32))
-        load_plane(nc.sync, tab_plane, tab_scales)
+        nc.sync.dma_start(out=tab_t[0][:], in_=words(tab_words, 0))
+        for q in range(4):
+            nc.sync.dma_start(
+                out=w4_plane_raw[32 * q : 32 * q + 4, :].bitcast(I32), in_=w4_scales[0, 4 * q : 4 * q + 4, :].bitcast(I32)
+            )
+        nc.sync.dma_start(out=offs2_t[:], in_=offs2)
+        load_rows(tab2_rows, tab2_scales)
         nc.sync.dma_start(out=tab_t[1][:], in_=words(tab_words, 1))
-        nc.sync.dma_start(out=w1_raw[0][:], in_=w1_rows[:, :, 0:HALF])
+
+        v_rows = sb("v_rows", [P, S], U8)
+        nc.vector.tensor_copy(out=v_rows[:], in_=tab_rows[:].indirect(offs_t[:]))
+        place_rows(v_plane[0], v_rows, 0)
         nc.sync.dma_start(out=gain_t[:], in_=gain.rearrange("(b p t) -> p b t", b=2, t=PACK))
+        nc.sync.dma_start(out=w1_raw[0][:], in_=w1_rows[:, :, 0:HALF])
+        place_rows(v_plane[1], v_rows, 1)
         nc.sync.dma_start(out=pos1_t[:], in_=pos1)
         nc.sync.dma_start(out=pos2_t[:], in_=pos2)
-        nc.sync.dma_start(out=offs2_t[:], in_=offs2)
         nc.sync.dma_start(out=w1_raw[1][:], in_=w1_rows[:, :, HALF:H])
         nc.sync.dma_start(out=d_t[:], in_=d.rearrange("(b p t) -> p b t", b=2, t=PACK))
-        load_plane(nc.sync, tab2_plane, tab2_scales)
         nc.sync.dma_start(out=tab2_t[0][:], in_=words(tab2_words, 0))
         nc.sync.dma_start(out=tab2_t[1][:], in_=words(tab2_words, 1))
-        nc.sync.dma_start(out=ref_t[:], in_=ref.rearrange("(m p) n -> p m n", p=P))
 
-        v_codes = [sb("v_codes0", [P, S], U32)]
+        v_codes = [sb("v_codes%d" % a, [P, S], U32) for a in range(2)]
         nc.vector.tensor_copy(out=v_codes[0][:], in_=tab_t[0][:].bitcast(U32).indirect(offs_t[:]))
-        w4_codes = sb("w4_codes", [P, H], U16)
-        nc.scalar.copy(
-            out=w4_codes[:].rearrange("p (b t m) -> p b m t", b=2, t=PACK),
-            in_=w4_raw[:].bitcast(U16).rearrange("p (b m t) -> p b m t", b=2, t=PACK),
-        )
         w4_plane = sb("w4_plane", [P, H], U8)
         nc.vector.tensor_copy(
             out=w4_plane[:].rearrange("p (b t m) -> p b m t", b=2, t=PACK),
             in_=w4_plane_raw[:].rearrange("p (b m t) -> p b m t", b=2, t=PACK),
         )
-        v_plane = sb("v_plane", [P, S], U8)
-        nc.vector.tensor_copy(out=v_plane[:], in_=tab_plane[:].indirect(offs_t[:]))
-        v_codes.append(sb("v_codes1", [P, S], U32, tag="tab_plane"))
+        v2_rows = sb("v2_rows", [P, S2], U8)
+        nc.vector.tensor_copy(out=v2_rows[:], in_=tab2_rows[:].indirect(offs2_t[:]))
+        for a in range(2):
+            place_rows(v2_plane, v2_rows, a)
+        nc.sync.dma_start(out=ref_t[:], in_=ref.rearrange("(m p) n -> p m n", p=P))
         nc.vector.tensor_copy(out=v_codes[1][:], in_=tab_t[1][:].bitcast(U32).indirect(offs_t[:]))
+        w4_codes = sb("w4_codes", [P, H], U16)
+        nc.scalar.copy(
+            out=w4_codes[:].rearrange("p (b t m) -> p b m t", b=2, t=PACK),
+            in_=w4_raw[:].bitcast(U16).rearrange("p (b m t) -> p b m t", b=2, t=PACK),
+        )
 
         w1_codes, w1_plane = {}, {}
 
-        def quantise_w1(b, copy):
-            grouped = sb("w1_grouped%d" % b, [P, 2, 2 * P * PACK], BF16, tag="tab1")
-            for u in range(2):
+        def quantise_w1(b, copy, slots):
+            grouped = sb("w1_grouped%d" % b, [P, PACK * P * PACK], BF16, tag="tab1")
+            for t0 in range(0, PACK, slots):
+                part = grouped[:, t0 * P * PACK : (t0 + slots) * P * PACK]
                 copy(
-                    out=grouped[:, u, :].rearrange("p (t m j) -> p m t j", t=2, j=PACK),
-                    in_=w1_raw[b][:].rearrange("p j (m t) -> p m t j", t=PACK)[:, :, 2 * u : 2 * u + 2, :],
+                    out=part.rearrange("p (t m j) -> p m j t", t=slots, j=PACK),
+                    in_=w1_raw[b][:].rearrange("p j (m t) -> p m j t", t=PACK)[:, :, :, t0 : t0 + slots],
                 )
-                w1_codes[b, u] = sb("w1_codes%d%d" % (b, u), [P, 2 * P], U32)
-                w1_plane[b, u] = sb("w1_plane%d%d" % (b, u), [P, 2 * P], U8)
-                nc.vector.quantize_mx(
-                    out=w1_codes[b, u][:].bitcast(FP8X4), scales=w1_plane[b, u][:], in_=grouped[:, u, :]
-                )
+                codes = sb("w1_codes%d%d" % (b, t0), [P, slots * P], U32)
+                plane = sb("w1_plane%d%d" % (b, t0), [P, slots * P], U8)
+                nc.vector.quantize_mx(out=codes[:].bitcast(FP8X4), scales=plane[:], in_=part)
+                for t in range(slots):
+                    w1_codes[b, t0 + t] = codes[:, P * t : P * (t + 1)]
+                    w1_plane[b, t0 + t] = plane[:, P * t : P * (t + 1)]
 
         z, h = {}, {}
 
@@ -130,41 +147,42 @@ def tile_list_handbag_authenticity_evidence_kernel(
                 views = slice(BANK * s, BANK * (s + 1))
                 nc.tensor.matmul_mx(
                     out=z[b, t, s][:], lhsT=w4_codes[:, cols].bitcast(FP4X4), lhsT_scale=w4_plane[:, cols],
-                    rhs=v_codes[0][:, views].bitcast(FP8X4), rhs_scale=v_plane[:, views], start=True, stop=False,
+                    rhs=v_codes[0][:, views].bitcast(FP8X4), rhs_scale=v_plane[0][:, views], start=True, stop=False,
                 )
 
         def w1_pass(b, t):
-            cols = slice(P * (t % 2), P * (t % 2 + 1))
             for s in range(2):
                 views = slice(BANK * s, BANK * (s + 1))
                 nc.tensor.matmul_mx(
-                    out=z[b, t, s][:], lhsT=w1_codes[b, t // 2][:, cols].bitcast(FP8X4),
-                    lhsT_scale=w1_plane[b, t // 2][:, cols],
-                    rhs=v_codes[1][:, views].bitcast(FP8X4), rhs_scale=v_plane[4:P, views], start=False, stop=True,
+                    out=z[b, t, s][:], lhsT=w1_codes[b, t].bitcast(FP8X4), lhsT_scale=w1_plane[b, t],
+                    rhs=v_codes[1][:, views].bitcast(FP8X4), rhs_scale=v_plane[1][4:P, views], start=False, stop=True,
                 )
 
         def evidence(b, t):
             h[b, t] = sb("h%d%d" % (b, t), [P, S], F32)
             g = gain_t[:, b, t : t + 1]
+            halves = [h[b, t][:, BANK * s : BANK * (s + 1)] for s in range(2)]
             for s in range(2):
-                views = slice(BANK * s, BANK * (s + 1))
-                nc.scalar.activation(out=h[b, t][:, views], in_=z[b, t, s][:], func=ACT.Tanh)
+                nc.scalar.activation(out=halves[s], in_=z[b, t, s][:], func=ACT.Tanh)
+            for half in halves:
                 if (b, t) == (0, 0):
-                    nc.vector.tensor_scalar(out=h[b, t][:, views], in0=h[b, t][:, views], scalar1=g, scalar2=None, op0=ALU.mult)
-            if (b, t) == (0, 0):
-                return
-            if (b, t) in GAIN_ON_VECTOR:
-                nc.vector.tensor_scalar(out=h[b, t][:], in0=h[b, t][:], scalar1=g, scalar2=None, op0=ALU.mult)
-            else:
-                nc.scalar.activation(out=h[b, t][:], in_=h[b, t][:], func=ACT.Copy, scale=g)
+                    nc.vector.tensor_scalar(out=half, in0=half, scalar1=g, scalar2=None, op0=ALU.mult)
+                else:
+                    nc.scalar.activation(out=half, in_=half, func=ACT.Copy, scale=g)
 
         def pick_handle(b, t):
-            nc.vector.tensor_copy(out=handle[b][:, t, :], in_=h[b, t][:].indirect(pos1_t[:]))
+            for s in range(2):
+                nc.vector.tensor_copy(
+                    out=handle[b][:, t, 256 * s : 256 * (s + 1)], in_=h[b, t][:].indirect(pos1_t[:, 16 * s : 16 * (s + 1)])
+                )
 
         def pick_lining(b, t):
-            nc.vector.tensor_tensor(
-                out=lining[b][:, t, :], in0=h[b, t][:].indirect(pos2_t[:]), in1=handle[b][:, t, :], op=ALU.subtract
-            )
+            for s in range(2):
+                cols = slice(256 * s, 256 * (s + 1))
+                nc.vector.tensor_tensor(
+                    out=lining[b][:, t, cols], in0=h[b, t][:].indirect(pos2_t[:, 16 * s : 16 * (s + 1)]),
+                    in1=handle[b][:, t, cols], op=ALU.subtract,
+                )
 
         def weave(copy, name, rows, width):
             woven = sb(name + "_woven", [P, PACK * width], BF16)
@@ -187,32 +205,30 @@ def tile_list_handbag_authenticity_evidence_kernel(
 
         for t in range(PACK):
             w4_pass(0, t)
-        quantise_w1(0, nc.vector.tensor_copy)
+        quantise_w1(0, nc.vector.tensor_copy, 2)
 
         handle = [sb("handle%d" % b, [P, PACK, N], F32) for b in range(2)]
-        lining = [sb("lining0", [P, PACK, N], F32)]
+        lining = [sb("lining%d" % b, [P, PACK, N], F32) for b in range(2)]
         for t in range(PACK):
             w1_pass(0, t)
             evidence(0, t)
             pick_handle(0, t)
             pick_lining(0, t)
             if t == 1:
-                quantise_w1(1, nc.scalar.copy)
-        v2_plane = sb("v2_plane", [P, S2], U8, tag="h00")
-        nc.vector.tensor_copy(out=v2_plane[:], in_=tab2_plane[:].indirect(offs2_t[:]))
+                quantise_w1(1, nc.scalar.copy, 4)
         v2_codes = []
         for a in range(2):
             v2_codes.append(sb("v2_codes%d" % a, [P, S2], U32, tag="h0%d" % (a + 1)))
             nc.vector.tensor_copy(out=v2_codes[a][:], in_=tab2_t[a][:].bitcast(U32).indirect(offs2_t[:]))
         for t in range(PACK):
+            if t == PACK - 1:
+                x1_0 = weave(nc.scalar.copy, "x1_0", scale_handle(0)[:], N)
             w4_pass(1, t)
             w1_pass(1, t)
             evidence(1, t)
             pick_handle(1, t)
-        scaled0 = scale_handle(0)
-        lining.append(sb("lining1", [P, PACK, N], F32, tag="handle0"))
-        for t in range(PACK):
             pick_lining(1, t)
+        x2_0 = weave(nc.scalar.copy, "x2_0", lining[0][:], N)
 
         def score_pass(banks, a, x, cols):
             codes, plane = x
@@ -229,8 +245,8 @@ def tile_list_handbag_authenticity_evidence_kernel(
                 )
 
         e1 = [bank(m, "e1_%d" % m) for m in range(4)]
-        score_pass(e1, 0, weave(nc.scalar.copy, "x1_0", scaled0[:], N), slice(0, N))
-        score_pass(e1, 1, weave(nc.scalar.copy, "x1_1", scale_handle(1)[:], N), slice(0, N))
+        score_pass(e1, 0, x1_0, slice(0, N))
+        score_pass(e1, 1, weave(nc.vector.tensor_copy, "x1_1", scale_handle(1)[:], N), slice(0, N))
         weighted = sb("weighted", [P, 4, N], F32)
         for m in range(4):
             nc.vector.tensor_tensor(out=weighted[:, m, :], in0=e1[m][:], in1=ref_t[:, m, :], op=ALU.mult)
@@ -239,9 +255,8 @@ def tile_list_handbag_authenticity_evidence_kernel(
         for c, (n0, width) in enumerate(CHUNKS):
             first = 4 + 4 * n0 // BANK
             e2.append([bank(first + i, "e2_%d%d" % (c, i)) for i in range(4 * width // BANK)])
-        x2 = weave(nc.scalar.copy, "x2_0", lining[0][:], N)
         for c, (n0, width) in enumerate(CHUNKS):
-            score_pass(e2[c], 0, x2, slice(n0, n0 + width))
+            score_pass(e2[c], 0, x2_0, slice(n0, n0 + width))
 
         out_rows = out.rearrange("(m p) n -> p m n", p=P)
         for c, (n0, width) in enumerate(CHUNKS):

@@ -18,7 +18,6 @@ PACK = 4
 H, T, S, T3, S2, N = 1024, 4096, 1024, 2048, 512, 512
 HALF = 512
 BANK = 512
-CHUNKS = ((0, 256), (256, 128), (384, 128))
 
 FLOPS = 2 * 1024 * H * S + 2 * 2 * H * S2 * N
 
@@ -92,12 +91,12 @@ def tile_list_handbag_authenticity_evidence_kernel(
         v_rows = sb("v_rows", [P, S], U8)
         nc.vector.tensor_copy(out=v_rows[:], in_=tab_rows[:].indirect(offs_t[:]))
         place_rows(v_plane[0], v_rows, 0)
-        nc.sync.dma_start(out=gain_t[:], in_=gain.rearrange("(b p t) -> p b t", b=2, t=PACK))
         nc.sync.dma_start(out=w1_raw[0][:], in_=w1_rows[:, :, 0:HALF])
         place_rows(v_plane[1], v_rows, 1)
+        nc.sync.dma_start(out=gain_t[:], in_=gain.rearrange("(b p t) -> p b t", b=2, t=PACK))
         nc.sync.dma_start(out=pos1_t[:], in_=pos1)
-        nc.sync.dma_start(out=pos2_t[:], in_=pos2)
         nc.sync.dma_start(out=w1_raw[1][:], in_=w1_rows[:, :, HALF:H])
+        nc.sync.dma_start(out=pos2_t[:], in_=pos2)
         nc.sync.dma_start(out=d_t[:], in_=d.rearrange("(b p t) -> p b t", b=2, t=PACK))
         nc.sync.dma_start(out=tab2_t[0][:], in_=words(tab2_words, 0))
         nc.sync.dma_start(out=tab2_t[1][:], in_=words(tab2_words, 1))
@@ -123,20 +122,18 @@ def tile_list_handbag_authenticity_evidence_kernel(
 
         w1_codes, w1_plane = {}, {}
 
-        def quantise_w1(b, copy, slots):
-            grouped = sb("w1_grouped%d" % b, [P, PACK * P * PACK], BF16, tag="tab1")
-            for t0 in range(0, PACK, slots):
-                part = grouped[:, t0 * P * PACK : (t0 + slots) * P * PACK]
-                copy(
-                    out=part.rearrange("p (t m j) -> p m j t", t=slots, j=PACK),
-                    in_=w1_raw[b][:].rearrange("p j (m t) -> p m j t", t=PACK)[:, :, :, t0 : t0 + slots],
-                )
-                codes = sb("w1_codes%d%d" % (b, t0), [P, slots * P], U32)
-                plane = sb("w1_plane%d%d" % (b, t0), [P, slots * P], U8)
-                nc.vector.quantize_mx(out=codes[:].bitcast(FP8X4), scales=plane[:], in_=part)
-                for t in range(slots):
-                    w1_codes[b, t0 + t] = codes[:, P * t : P * (t + 1)]
-                    w1_plane[b, t0 + t] = plane[:, P * t : P * (t + 1)]
+        def quantise_w1(grouped, b, t0, copy):
+            part = grouped[:, t0 * P * PACK : (t0 + 2) * P * PACK]
+            copy(
+                out=part.rearrange("p (t m j) -> p m j t", t=2, j=PACK),
+                in_=w1_raw[b][:].rearrange("p j (m t) -> p m j t", t=PACK)[:, :, :, t0 : t0 + 2],
+            )
+            codes = sb("w1_codes%d%d" % (b, t0), [P, 2 * P], U32)
+            plane = sb("w1_plane%d%d" % (b, t0), [P, 2 * P], U8)
+            nc.vector.quantize_mx(out=codes[:].bitcast(FP8X4), scales=plane[:], in_=part)
+            for t in range(2):
+                w1_codes[b, t0 + t] = codes[:, P * t : P * (t + 1)]
+                w1_plane[b, t0 + t] = plane[:, P * t : P * (t + 1)]
 
         z, h = {}, {}
 
@@ -205,7 +202,11 @@ def tile_list_handbag_authenticity_evidence_kernel(
 
         for t in range(PACK):
             w4_pass(0, t)
-        quantise_w1(0, nc.vector.tensor_copy, 2)
+        grouped = sb("w1_grouped0", [P, PACK * P * PACK], BF16, tag="tab1")
+        for t0 in (0, 2):
+            quantise_w1(grouped, 0, t0, nc.vector.tensor_copy)
+        grouped = sb("w1_grouped1", [P, PACK * P * PACK], BF16, tag="tab1")
+        quantise_w1(grouped, 1, 0, nc.vector.tensor_copy)
 
         handle = [sb("handle%d" % b, [P, PACK, N], F32) for b in range(2)]
         lining = [sb("lining%d" % b, [P, PACK, N], F32) for b in range(2)]
@@ -215,7 +216,7 @@ def tile_list_handbag_authenticity_evidence_kernel(
             pick_handle(0, t)
             pick_lining(0, t)
             if t == 1:
-                quantise_w1(1, nc.scalar.copy, 4)
+                quantise_w1(grouped, 1, 2, nc.scalar.copy)
         v2_codes = []
         for a in range(2):
             v2_codes.append(sb("v2_codes%d" % a, [P, S2], U32, tag="h0%d" % (a + 1)))
@@ -230,45 +231,38 @@ def tile_list_handbag_authenticity_evidence_kernel(
             pick_lining(1, t)
         x2_0 = weave(nc.scalar.copy, "x2_0", lining[0][:], N)
 
-        def score_pass(banks, a, x, cols):
+        def score_pass(banks, a, x, n0, width, start, stop):
             codes, plane = x
-            width = cols.stop - cols.start
-            per_bank = BANK // width
             for m in range(4):
                 rows = slice(P * m, P * (m + 1))
-                k = m % per_bank
                 nc.tensor.matmul_mx(
-                    out=banks[m // per_bank][:, k * width : (k + 1) * width],
+                    out=banks[m][:, n0 : n0 + width],
                     lhsT=v2_codes[a][:, rows].bitcast(FP8X4), lhsT_scale=v2_plane[4 * a : P, rows],
-                    rhs=codes[:, cols].bitcast(FP8X4), rhs_scale=plane[:, cols],
-                    start=(a == 0 and k == 0), stop=(a == 1 and k == per_bank - 1),
+                    rhs=codes[:].bitcast(FP8X4), rhs_scale=plane[:], start=start, stop=stop,
                 )
 
         e1 = [bank(m, "e1_%d" % m) for m in range(4)]
-        score_pass(e1, 0, x1_0, slice(0, N))
-        score_pass(e1, 1, weave(nc.vector.tensor_copy, "x1_1", scale_handle(1)[:], N), slice(0, N))
-        weighted = sb("weighted", [P, 4, N], F32)
-        for m in range(4):
-            nc.vector.tensor_tensor(out=weighted[:, m, :], in0=e1[m][:], in1=ref_t[:, m, :], op=ALU.mult)
+        e2 = [bank(4 + m, "e2_%d" % m) for m in range(4)]
+        score_pass(e1, 0, x1_0, 0, N, True, False)
+        score_pass(e2, 0, x2_0, 0, N, True, False)
+        score_pass(e1, 1, weave(nc.vector.tensor_copy, "x1_1", scale_handle(1)[:], N), 0, N, False, True)
+        for s in range(2):
+            x2_1 = weave(nc.scalar.copy, "x2_1%d" % s, lining[1][:, :, 256 * s : 256 * (s + 1)], 256)
+            score_pass(e2, 1, x2_1, 256 * s, 256, False, s == 1)
 
-        e2 = []
-        for c, (n0, width) in enumerate(CHUNKS):
-            first = 4 + 4 * n0 // BANK
-            e2.append([bank(first + i, "e2_%d%d" % (c, i)) for i in range(4 * width // BANK)])
-        for c, (n0, width) in enumerate(CHUNKS):
-            score_pass(e2[c], 0, x2_0, slice(n0, n0 + width))
+        weighted = [sb("weighted%d" % m, [P, N], F32) for m in range(4)]
 
-        out_rows = out.rearrange("(m p) n -> p m n", p=P)
-        for c, (n0, width) in enumerate(CHUNKS):
-            cols = slice(n0, n0 + width)
-            x2 = weave(nc.scalar.copy, "x2_1%d" % c, lining[1][:, :, cols], width)
-            score_pass(e2[c], 1, x2, slice(0, width))
-            per_bank = BANK // width
-            for i in range(len(e2[c])):
-                rows = slice(per_bank * i, per_bank * (i + 1))
-                result = sb("result%d%d" % (c, i), [P, per_bank, width], F32)
-                nc.vector.tensor_tensor(
-                    out=result[:], in0=e2[c][i][:].rearrange("p (m n) -> p m n", n=width),
-                    in1=weighted[:, rows, cols], op=ALU.add,
-                )
-                nc.sync.dma_start(out=out_rows[:, rows, cols], in_=result[:])
+        def weigh(m):
+            nc.vector.tensor_tensor(out=weighted[m][:], in0=e1[m][:], in1=ref_t[:, m, :], op=ALU.mult)
+
+        def finish(m, cols):
+            result = sb("result%d_%d" % (m, cols.start), [P, cols.stop - cols.start], F32)
+            nc.vector.tensor_tensor(out=result[:], in0=e2[m][:, cols], in1=weighted[m][:, cols], op=ALU.add)
+            nc.sync.dma_start(out=out[P * m : P * (m + 1), cols], in_=result[:])
+
+        weigh(0)
+        for m in range(3):
+            weigh(m + 1)
+            finish(m, slice(0, N))
+        for s in range(2):
+            finish(3, slice(256 * s, 256 * (s + 1)))

from contextlib import ExitStack

import concourse.mybir as mybir

F32 = mybir.dt.float32
BF16 = mybir.dt.bfloat16
I32 = mybir.dt.int32
U32 = mybir.dt.uint32
U16 = mybir.dt.uint16
U8 = mybir.dt.uint8
FP8X4 = mybir.dt.float8_e4m3fn_x4
FP4X4 = mybir.dt.float4_e2m1fn_x4
ACT = mybir.ActivationFunctionType
ALU = mybir.AluOpType

P = 128
PACK = 4
H, T, S, T3, S2, N = 1024, 4096, 1024, 2048, 512, 512
HALF = 512
BANK = 512

FLOPS = 2 * 1024 * H * S + 2 * 2 * H * S2 * N


def tile_list_handbag_authenticity_evidence_kernel(
    tc, tab_words, tab_scales, tab2_words, tab2_scales, w4_words, w4_scales, w1, gain, d, ref,
    offs, offs2, pos1, pos2, out,
):
    nc = tc.nc
    with ExitStack() as ctx:
        lists = ctx.enter_context(tc.tile_pool(name="lists", bufs=1))
        keep = ctx.enter_context(tc.tile_pool(name="keep", bufs=1))
        psum = ctx.enter_context(tc.psum_pool(name="psum", bufs=1))

        def sb(name, shape, dtype, tag=None):
            return keep.tile(shape, dtype, name=name, tag=tag or name, align_bytes=64)

        def bank(i, name):
            return psum.tile([P, BANK], F32, name=name, tag="bank%d" % i)

        offs_t = lists.tile([P, S // 16], U16, name="offs_t")
        offs2_t = lists.tile([P, S2 // 16], U16, name="offs2_t")
        pos1_t = lists.tile([P, N // 16], U16, name="pos1_t")
        pos2_t = lists.tile([P, N // 16], U16, name="pos2_t")

        tab_rows = sb("tab_rows", [P, T], U8)
        tab2_rows = sb("tab2_rows", [P, T3], U8)
        w4_plane_raw = sb("w4_plane_raw", [P, H], U8)
        v_plane = [sb("v_plane%d" % a, [P, S], U8) for a in range(2)]
        v2_plane = sb("v2_plane", [P, S2], U8)
        nc.vector.memset(w4_plane_raw[:].bitcast(I32), 0)
        for rows in (tab_rows, tab2_rows):
            nc.vector.memset(rows[0:96, :].bitcast(I32), 0)
        for plane in (v_plane[0], v_plane[1], v2_plane):
            nc.vector.memset(plane[:].bitcast(I32), 0)

        tab_t = [sb("tab%d" % a, [P, T], I32) for a in range(2)]
        tab2_t = [sb("tab2_%d" % a, [P, T3], I32) for a in range(2)]
        w4_raw = sb("w4_raw", [P, H // 2], I32)
        w1_raw = [sb("w1_raw%d" % b, [P, PACK, HALF], F32) for b in range(2)]
        ref_t = sb("ref_t", [P, 4, N], F32)
        gain_t = sb("gain_t", [P, 2, PACK], F32)
        d_t = sb("d_t", [P, 2, PACK], F32)

        def words(table, a):
            return table[a].rearrange("p n t -> p (n t)").bitcast(I32)

        w1_rows = w1.rearrange("(p j) c -> p j c", j=PACK)
        def load_rows(rows, scales):
            nc.sync.dma_start(out=rows[96:P, :].bitcast(I32), in_=scales.rearrange("a q t -> (a q) t").bitcast(I32))

        def place_rows(plane, picked, a):
            for q in range(4):
                nc.sync.dma_start(
                    out=plane[32 * q + 4 * a : 32 * q + 4 * a + 4, :].bitcast(I32),
                    in_=picked[96 + 16 * a + 4 * q : 96 + 16 * a + 4 * q + 4, :].bitcast(I32),
                )

        nc.sync.dma_start(out=offs_t[:], in_=offs)
        load_rows(tab_rows, tab_scales)
        nc.sync.dma_start(out=w4_raw[:], in_=w4_words[0].bitcast(I32))
        nc.sync.dma_start(out=tab_t[0][:], in_=words(tab_words, 0))
        for q in range(4):
            nc.sync.dma_start(
                out=w4_plane_raw[32 * q : 32 * q + 4, :].bitcast(I32), in_=w4_scales[0, 4 * q : 4 * q + 4, :].bitcast(I32)
            )
        nc.sync.dma_start(out=offs2_t[:], in_=offs2)
        load_rows(tab2_rows, tab2_scales)
        nc.sync.dma_start(out=tab_t[1][:], in_=words(tab_words, 1))

        v_rows = sb("v_rows", [P, S], U8)
        nc.vector.tensor_copy(out=v_rows[:], in_=tab_rows[:].indirect(offs_t[:]))
        place_rows(v_plane[0], v_rows, 0)
        nc.sync.dma_start(out=w1_raw[0][:], in_=w1_rows[:, :, 0:HALF])
        place_rows(v_plane[1], v_rows, 1)
        nc.sync.dma_start(out=gain_t[:], in_=gain.rearrange("(b p t) -> p b t", b=2, t=PACK))
        nc.sync.dma_start(out=pos1_t[:], in_=pos1)
        nc.sync.dma_start(out=w1_raw[1][:], in_=w1_rows[:, :, HALF:H])
        nc.sync.dma_start(out=pos2_t[:], in_=pos2)
        nc.sync.dma_start(out=d_t[:], in_=d.rearrange("(b p t) -> p b t", b=2, t=PACK))
        nc.sync.dma_start(out=tab2_t[0][:], in_=words(tab2_words, 0))
        nc.sync.dma_start(out=tab2_t[1][:], in_=words(tab2_words, 1))

        v_codes = [sb("v_codes%d" % a, [P, S], U32) for a in range(2)]
        nc.vector.tensor_copy(out=v_codes[0][:], in_=tab_t[0][:].bitcast(U32).indirect(offs_t[:]))
        w4_plane = sb("w4_plane", [P, H], U8)
        nc.vector.tensor_copy(
            out=w4_plane[:].rearrange("p (b t m) -> p b m t", b=2, t=PACK),
            in_=w4_plane_raw[:].rearrange("p (b m t) -> p b m t", b=2, t=PACK),
        )
        v2_rows = sb("v2_rows", [P, S2], U8)
        nc.vector.tensor_copy(out=v2_rows[:], in_=tab2_rows[:].indirect(offs2_t[:]))
        for a in range(2):
            place_rows(v2_plane, v2_rows, a)
        nc.sync.dma_start(out=ref_t[:], in_=ref.rearrange("(m p) n -> p m n", p=P))
        nc.vector.tensor_copy(out=v_codes[1][:], in_=tab_t[1][:].bitcast(U32).indirect(offs_t[:]))
        w4_codes = sb("w4_codes", [P, H], U16)
        nc.scalar.copy(
            out=w4_codes[:].rearrange("p (b t m) -> p b m t", b=2, t=PACK),
            in_=w4_raw[:].bitcast(U16).rearrange("p (b m t) -> p b m t", b=2, t=PACK),
        )

        w1_codes, w1_plane = {}, {}

        def quantise_w1(grouped, b, t0, copy):
            part = grouped[:, t0 * P * PACK : (t0 + 2) * P * PACK]
            copy(
                out=part.rearrange("p (t m j) -> p m j t", t=2, j=PACK),
                in_=w1_raw[b][:].rearrange("p j (m t) -> p m j t", t=PACK)[:, :, :, t0 : t0 + 2],
            )
            codes = sb("w1_codes%d%d" % (b, t0), [P, 2 * P], U32)
            plane = sb("w1_plane%d%d" % (b, t0), [P, 2 * P], U8)
            nc.vector.quantize_mx(out=codes[:].bitcast(FP8X4), scales=plane[:], in_=part)
            for t in range(2):
                w1_codes[b, t0 + t] = codes[:, P * t : P * (t + 1)]
                w1_plane[b, t0 + t] = plane[:, P * t : P * (t + 1)]

        z, h = {}, {}

        def w4_pass(b, t):
            cols = slice(HALF * b + P * t, HALF * b + P * (t + 1))
            for s in range(2):
                z[b, t, s] = bank(2 * t + s, "z%d%d%d" % (b, t, s))
                views = slice(BANK * s, BANK * (s + 1))
                nc.tensor.matmul_mx(
                    out=z[b, t, s][:], lhsT=w4_codes[:, cols].bitcast(FP4X4), lhsT_scale=w4_plane[:, cols],
                    rhs=v_codes[0][:, views].bitcast(FP8X4), rhs_scale=v_plane[0][:, views], start=True, stop=False,
                )

        def w1_pass(b, t):
            for s in range(2):
                views = slice(BANK * s, BANK * (s + 1))
                nc.tensor.matmul_mx(
                    out=z[b, t, s][:], lhsT=w1_codes[b, t].bitcast(FP8X4), lhsT_scale=w1_plane[b, t],
                    rhs=v_codes[1][:, views].bitcast(FP8X4), rhs_scale=v_plane[1][4:P, views], start=False, stop=True,
                )

        def evidence(b, t):
            h[b, t] = sb("h%d%d" % (b, t), [P, S], F32)
            g = gain_t[:, b, t : t + 1]
            halves = [h[b, t][:, BANK * s : BANK * (s + 1)] for s in range(2)]
            for s in range(2):
                nc.scalar.activation(out=halves[s], in_=z[b, t, s][:], func=ACT.Tanh)
            for half in halves:
                if (b, t) == (0, 0):
                    nc.vector.tensor_scalar(out=half, in0=half, scalar1=g, scalar2=None, op0=ALU.mult)
                else:
                    nc.scalar.activation(out=half, in_=half, func=ACT.Copy, scale=g)

        def pick_handle(b, t):
            for s in range(2):
                nc.vector.tensor_copy(
                    out=handle[b][:, t, 256 * s : 256 * (s + 1)], in_=h[b, t][:].indirect(pos1_t[:, 16 * s : 16 * (s + 1)])
                )

        def pick_lining(b, t):
            for s in range(2):
                cols = slice(256 * s, 256 * (s + 1))
                nc.vector.tensor_tensor(
                    out=lining[b][:, t, cols], in0=h[b, t][:].indirect(pos2_t[:, 16 * s : 16 * (s + 1)]),
                    in1=handle[b][:, t, cols], op=ALU.subtract,
                )

        def weave(copy, name, rows, width):
            woven = sb(name + "_woven", [P, PACK * width], BF16)
            copy(
                out=woven[:].rearrange("p (c i t) -> p c t i", i=PACK, t=PACK),
                in_=rows.rearrange("p t (c i) -> p c t i", i=PACK),
            )
            codes = sb(name + "_codes", [P, width], U32)
            plane = sb(name + "_plane", [P, width], U8)
            nc.vector.quantize_mx(out=codes[:].bitcast(FP8X4), scales=plane[:], in_=woven[:])
            return codes, plane

        def scale_handle(b):
            scaled = sb("scaled%d" % b, [P, PACK, N], BF16)
            for t in range(PACK):
                nc.scalar.activation(
                    out=scaled[:, t, :], in_=handle[b][:, t, :], func=ACT.Copy, scale=d_t[:, b, t : t + 1]
                )
            return scaled

        for t in range(PACK):
            w4_pass(0, t)
        grouped = sb("w1_grouped0", [P, PACK * P * PACK], BF16, tag="tab1")
        for t0 in (0, 2):
            quantise_w1(grouped, 0, t0, nc.vector.tensor_copy)
        grouped = sb("w1_grouped1", [P, PACK * P * PACK], BF16, tag="tab1")
        quantise_w1(grouped, 1, 0, nc.vector.tensor_copy)

        handle = [sb("handle%d" % b, [P, PACK, N], F32) for b in range(2)]
        lining = [sb("lining%d" % b, [P, PACK, N], F32) for b in range(2)]
        for t in range(PACK):
            w1_pass(0, t)
            evidence(0, t)
            pick_handle(0, t)
            pick_lining(0, t)
            if t == 1:
                quantise_w1(grouped, 1, 2, nc.scalar.copy)
        v2_codes = []
        for a in range(2):
            v2_codes.append(sb("v2_codes%d" % a, [P, S2], U32, tag="h0%d" % (a + 1)))
            nc.vector.tensor_copy(out=v2_codes[a][:], in_=tab2_t[a][:].bitcast(U32).indirect(offs2_t[:]))
        for t in range(PACK):
            if t == PACK - 1:
                x1_0 = weave(nc.scalar.copy, "x1_0", scale_handle(0)[:], N)
            w4_pass(1, t)
            w1_pass(1, t)
            evidence(1, t)
            pick_handle(1, t)
            pick_lining(1, t)
        x2_0 = weave(nc.scalar.copy, "x2_0", lining[0][:], N)

        def score_pass(banks, a, x, n0, width, start, stop):
            codes, plane = x
            for m in range(4):
                rows = slice(P * m, P * (m + 1))
                nc.tensor.matmul_mx(
                    out=banks[m][:, n0 : n0 + width],
                    lhsT=v2_codes[a][:, rows].bitcast(FP8X4), lhsT_scale=v2_plane[4 * a : P, rows],
                    rhs=codes[:].bitcast(FP8X4), rhs_scale=plane[:], start=start, stop=stop,
                )

        e1 = [bank(m, "e1_%d" % m) for m in range(4)]
        e2 = [bank(4 + m, "e2_%d" % m) for m in range(4)]
        score_pass(e1, 0, x1_0, 0, N, True, False)
        score_pass(e2, 0, x2_0, 0, N, True, False)
        score_pass(e1, 1, weave(nc.vector.tensor_copy, "x1_1", scale_handle(1)[:], N), 0, N, False, True)
        for s in range(2):
            x2_1 = weave(nc.scalar.copy, "x2_1%d" % s, lining[1][:, :, 256 * s : 256 * (s + 1)], 256)
            score_pass(e2, 1, x2_1, 256 * s, 256, False, s == 1)

        weighted = [sb("weighted%d" % m, [P, N], F32) for m in range(4)]

        def weigh(m):
            nc.vector.tensor_tensor(out=weighted[m][:], in0=e1[m][:], in1=ref_t[:, m, :], op=ALU.mult)

        def finish(m, cols):
            result = sb("result%d_%d" % (m, cols.start), [P, cols.stop - cols.start], F32)
            nc.vector.tensor_tensor(out=result[:], in0=e2[m][:, cols], in1=weighted[m][:, cols], op=ALU.add)
            nc.sync.dma_start(out=out[P * m : P * (m + 1), cols], in_=result[:])

        weigh(0)
        for m in range(3):
            weigh(m + 1)
            finish(m, slice(0, N))
        for s in range(2):
            finish(3, slice(256 * s, 256 * (s + 1)))
